import numpy as np
import ml_dtypes


def mxq(x, axis, fmt="e4m3"):
    dtype, down = {"e4m3": (ml_dtypes.float8_e4m3fn, 7), "e5m2": (ml_dtypes.float8_e5m2, 14)}[fmt]
    v = np.moveaxis(np.asarray(x, np.float32).astype(ml_dtypes.bfloat16).astype(np.float64), axis, -1)
    blocks = v.reshape(v.shape[:-1] + (-1, 32))
    amax = np.abs(blocks).max(-1, keepdims=True)
    byte = np.maximum(np.where(amax > 0, np.frexp(amax)[1] - 1 + 127, 0) - down, 1)
    scale = np.exp2(byte - 127.0)
    codes = (blocks / scale).astype(np.float32).astype(dtype).astype(np.float64)
    return np.moveaxis((codes * scale).reshape(v.shape), -1, axis)


WIDE = False


def mx_kscale(k):
    if not WIDE:
        return np.ones(k)
    levels = np.array([10, -10, 5, -5, 0])
    if k % 512:
        return np.exp2(np.random.permutation(np.resize(levels, k // 32))).repeat(32)
    a = np.empty((k // 512, 16))
    for p in range(k // 512):
        a[p, :8] = np.random.permutation(np.resize(levels, 8))
        for g in range(8):
            far = levels[np.abs(levels - a[p, g]) >= 10]
            a[p, g + 8] = far[np.random.randint(len(far))]
    return np.exp2(a.ravel()).repeat(32)


def f64(x):
    return np.asarray(x).astype(np.float64)


E2M1 = np.array([0.0, 0.5, 1.0, 1.5, 2.0, 3.0, 4.0, 6.0, -0.0, -0.5, -1.0, -1.5, -2.0, -3.0, -4.0, -6.0])


def pack_weight(w, fmt):
    k, n = w.shape
    w = f64(np.asarray(w, np.float32).astype(ml_dtypes.bfloat16)).reshape(k // 32, 32, n)
    amax = np.abs(w).max(1)
    if fmt == "e4m3":
        byte = np.frexp(amax)[1] - 1 + 127 - 7
    else:
        mant, ex = np.frexp(amax / 6.0)
        byte = np.where(mant > 0.5, ex, ex - 1) + 127
    byte = np.clip(np.where(amax > 0, byte, 1), 1, 254)
    scaled = (w * np.exp2(127.0 - byte)[:, None, :]).reshape(k, n).astype(np.float32)
    by_word = np.ascontiguousarray(scaled.reshape(k // 512, 128, 4, n).transpose(0, 1, 3, 2))
    if fmt == "e4m3":
        words = by_word.astype(ml_dtypes.float8_e4m3fn).view(np.uint8)
    else:
        c = by_word.astype(ml_dtypes.float4_e2m1fn).view(np.uint8) & 0xF
        words = (c[..., 0::2] | (c[..., 1::2] << 4)).reshape(k // 512, 128, 2 * n)
    return np.ascontiguousarray(words), np.ascontiguousarray(byte.astype(np.uint8).reshape(k // 512, 16, n))


def unpack_weight(words, scales, fmt):
    g, _, n = scales.shape
    words = np.ascontiguousarray(words).reshape(g, 128, n, -1)
    if fmt == "e4m3":
        vals = words.view(ml_dtypes.float8_e4m3fn).astype(np.float64)
    else:
        nib = np.empty((g, 128, n, 4), np.uint8)
        nib[..., 0::2] = words & 0xF
        nib[..., 1::2] = words >> 4
        vals = E2M1[nib]
    vals = vals * np.repeat(np.exp2(scales.astype(np.float64) - 127.0), 8, axis=1)[..., None]
    return vals.transpose(0, 1, 3, 2).reshape(g * 512, n)


K, L, Q, I, N = 512, 512, 512, 512, 512


def setup_inputs():
    n = np.random.standard_normal
    fk = mx_kscale(K)
    fl = mx_kscale(L)
    fi = mx_kscale(I)
    qap = pack_weight(n((K, Q)) * 0.06 * fk[:, None], "e4m3")
    kap = pack_weight(n((K, I)) / fk[:, None], "e2m1")
    qbp = pack_weight(n((L, Q)) * 0.06 * fl[:, None], "e4m3")
    kbp = pack_weight(n((L, I)) / fl[:, None], "e2m1")
    vop = pack_weight(n((I, N)) * 1 / np.sqrt(I) / fi[:, None], "e4m3")
    wyp = pack_weight(n((K, N)) * 10.0 / np.sqrt(K) / fk[:, None], "e2m1")
    return {
        "qa_words": qap[0],
        "qa_scales": qap[1],
        "ka_words": kap[0],
        "ka_scales": kap[1],
        "qb_words": qbp[0],
        "qb_scales": qbp[1],
        "kb_words": kbp[0],
        "kb_scales": kbp[1],
        "fi": (np.random.uniform(0.5, 2.0, (I, 1)) * fi[:, None]).astype(np.float32),
        "vo_words": vop[0],
        "vo_scales": vop[1],
        "wy_words": wyp[0],
        "wy_scales": wyp[1],
    }


def reference(qa_words, qa_scales, ka_words, ka_scales, qb_words, qb_scales, kb_words, kb_scales, fi, vo_words, vo_scales, wy_words, wy_scales):
    qau = unpack_weight(qa_words, qa_scales, "e4m3")
    kau = unpack_weight(ka_words, ka_scales, "e2m1")
    qbu = unpack_weight(qb_words, qb_scales, "e4m3")
    kbu = unpack_weight(kb_words, kb_scales, "e2m1")
    vou = unpack_weight(vo_words, vo_scales, "e4m3")
    wyu = unpack_weight(wy_words, wy_scales, "e2m1")
    a = qau.T @ kau + qbu.T @ kbu
    p = np.maximum(a, 0.0)
    pt = p.T
    pw = pt * f64(fi)
    pwq = mxq(pw, 0, "e4m3")
    y = vou.T @ pwq + wyu.T @ qau
    return y

@@ -1,0 +1,173 @@
+from contextlib import ExitStack
+
+import concourse.mybir as mybir
+
+F32 = mybir.dt.float32
+BF16 = mybir.dt.bfloat16
+I32 = mybir.dt.int32
+U32 = mybir.dt.uint32
+U8 = mybir.dt.uint8
+FP8X4 = mybir.dt.float8_e4m3fn_x4
+FP4X4 = mybir.dt.float4_e2m1fn_x4
+ALU = mybir.AluOpType
+
+P = 128
+W = 512
+PACK = 4
+CH = 128
+FLOPS = 4 * 2 * 512 * 512 * 512
+
+
+def tile_mix_positive_scores_carry_rows_kernel(
+    tc, qa_words, qa_scales, ka_words, ka_scales, qb_words, qb_scales, kb_words, kb_scales,
+    fi, vo_words, vo_scales, wy_words, wy_scales, out,
+):
+    nc = tc.nc
+    with ExitStack() as ctx:
+        sb = ctx.enter_context(tc.tile_pool(name="sb", bufs=1))
+        psum = ctx.enter_context(tc.psum_pool(name="psum", bufs=1))
+        ctx.enter_context(tc.manual_schedule())
+
+        def fp8_tile(name):
+            return sb.tile([P, W], U32, name=name, align_bytes=64)
+
+        def byte_tile(name, width):
+            return sb.tile([P, width], U8, name=name, align_bytes=64)
+
+        qa, qb, vo, pw = fp8_tile("qa"), fp8_tile("qb"), fp8_tile("vo"), fp8_tile("pw")
+        ka_raw, kb_raw, wy = byte_tile("ka_raw", 2 * W), byte_tile("kb_raw", 2 * W), byte_tile("wy", 2 * W)
+        ka, kb = byte_tile("ka", 2 * W), byte_tile("kb", 2 * W)
+        planes = byte_tile("planes", 6 * W)
+        ka_s_raw, qa_s, kb_s_raw, qb_s, wy_s, vo_s = [planes[:, W * n : W * (n + 1)] for n in range(6)]
+        ka_s, kb_s, pw_s = byte_tile("ka_s", W), byte_tile("kb_s", W), byte_tile("pw_s", W)
+        fi_sb = sb.tile([P, PACK], F32, name="fi_sb")
+        pw_bf = [sb.tile([P, CH, PACK], BF16, name="pw_bf%d" % c, align_bytes=64) for c in range(4)]
+        y_sb = [sb.tile([P, 4, CH], F32, name="y_sb%d" % c) for c in range(4)]
+
+        def load_fp8(eng, tile, words):
+            eng.dma_start(out=tile[:].bitcast(I32), in_=words[0].rearrange("p n t -> p (n t)").bitcast(I32))
+
+        def load_fp4(eng, tile, words):
+            eng.dma_start(out=tile[:].bitcast(I32), in_=words[0].bitcast(I32))
+
+        def load_scale(eng, plane, scales, r):
+            eng.dma_start(out=plane.bitcast(I32)[r:P:32, :], in_=scales[0].bitcast(I32)[r:16:4, :])
+
+        def load_scale_all(eng, plane, scales):
+            src = scales[0].bitcast(I32).rearrange("(Q r) c -> Q (r c)", r=4).unsqueeze(1).to_broadcast([4, 8, W])
+            eng.dma_start(out=plane.bitcast(I32), in_=src)
+
+        def regroup_words(dst, src):
+            nc.vector.tensor_copy(
+                out=dst[:].rearrange("p (t m b) -> p t m b", t=PACK, b=2),
+                in_=src[:].rearrange("p (m t b) -> p t m b", t=PACK, b=2),
+            )
+
+        def regroup_scales(dst, src):
+            nc.vector.tensor_copy(
+                out=dst[:].rearrange("p (t m) -> p t m", t=PACK),
+                in_=src.rearrange("p (m t) -> p t m", t=PACK),
+            )
+
+        def cols(c):
+            return slice(CH * c, CH * (c + 1))
+
+        def passes(bank, js, w, w_s, w_fp4, x, x_s, c, start, stop):
+            for n, j in enumerate(js):
+                if w_fp4:
+                    lhsT = w[:, 2 * P * j : 2 * P * (j + 1)].bitcast(FP4X4)
+                else:
+                    lhsT = w[:, cols(j)].bitcast(FP8X4)
+                nc.tensor.matmul_mx(
+                    out=bank[:, n, :], lhsT=lhsT, lhsT_scale=w_s[:, cols(j)],
+                    rhs=x[:, cols(c)].bitcast(FP8X4), rhs_scale=x_s[:, cols(c)],
+                    start=start and n == 0, stop=stop and n == len(js) - 1,
+                )
+
+        def weigh(c):
+            nc.vector.scalar_tensor_tensor(
+                out=pw_bf[c][:], in0=a_bank[c][:].rearrange("p t q -> p q t"), scalar=0.0,
+                in1=fi_sb[:].unsqueeze(1).to_broadcast([P, CH, PACK]), op0=ALU.max, op1=ALU.mult,
+            )
+
+        def quantize(c):
+            nc.vector.quantize_mx(
+                out=pw[:, cols(c)].bitcast(FP8X4), scales=pw_s[:, cols(c)],
+                in_=pw_bf[c][:].rearrange("p q t -> p (q t)"),
+            )
+
+        out_v = out.rearrange("(j p) q -> p j q", p=P)
+        sy, sc, gp = nc.sync, nc.scalar, nc.gpsimd
+        ALL = [0, 1, 2, 3]
+
+        stage = byte_tile("stage", 6 * W)
+
+        def load_rows(eng, n, scales):
+            eng.dma_start(out=stage[0:16, W * n : W * (n + 1)].bitcast(I32), in_=scales[0].bitcast(I32))
+
+        def spread(eng, first, last, Q):
+            span = slice(W * first, W * last)
+            eng.dma_start(out=planes[32 * Q : 32 * Q + 4, span].bitcast(I32), in_=stage[4 * Q : 4 * Q + 4, span].bitcast(I32))
+
+        nc.vector.memset(planes[:].bitcast(I32), 0)
+        gp.dma_start(out=fi_sb[:], in_=fi.rearrange("(p t) o -> p (t o)", t=PACK))
+        load_rows(sy, 0, ka_scales)
+        load_rows(sc, 1, qa_scales)
+        load_rows(sy, 2, kb_scales)
+        load_rows(sc, 3, qb_scales)
+        load_fp4(sy, ka_raw, ka_words)
+        load_fp8(sc, qa, qa_words)
+        load_fp4(sy, kb_raw, kb_words)
+        load_fp8(sc, qb, qb_words)
+        for Q in range(4):
+            spread(sy if Q % 2 == 0 else sc, 0, 4, Q)
+        load_rows(sy, 4, wy_scales)
+        load_rows(sy, 5, vo_scales)
+        load_fp4(sy, wy, wy_words)
+        load_fp8(sy, vo, vo_words)
+        for Q in range(4):
+            spread(sy, 4, 6, Q)
+
+        a_bank = [psum.tile([P, PACK, CH], F32, name="a%d" % c) for c in range(4)]
+        y_bank = [psum.tile([P, 4, CH], F32, name="y%d" % c) for c in range(3)]
+        y_lo = psum.tile([P, 2, CH], F32, name="y3")
+
+        regroup_words(ka, ka_raw)
+        regroup_words(kb, kb_raw)
+        regroup_scales(ka_s, ka_s_raw)
+        regroup_scales(kb_s, kb_s_raw)
+        for c in range(4):
+            passes(a_bank[c], ALL, ka, ka_s, True, qa, qa_s, c, True, False)
+            passes(a_bank[c], ALL, kb, kb_s, True, qb, qb_s, c, False, True)
+
+        def skip(c):
+            passes(y_bank[c], ALL, wy, wy_s, True, qa, qa_s, c, True, False)
+
+        def carry(c):
+            passes(y_bank[c], ALL, vo, vo_s, False, pw, pw_s, c, False, True)
+            nc.scalar.copy(out=y_sb[c][:], in_=y_bank[c][:])
+            sy.dma_start(out=out_v[:, :, cols(c)], in_=y_sb[c][:])
+
+        weigh(0)
+        y_hi = psum.tile([P, 2, CH], F32, name="a0")
+        weigh(1)
+        quantize(0)
+        skip(0)
+        skip(1)
+        carry(0)
+        weigh(2)
+        quantize(1)
+        skip(2)
+        carry(1)
+        weigh(3)
+        quantize(2)
+        passes(y_lo, [0, 1], wy, wy_s, True, qa, qa_s, 3, True, False)
+        passes(y_hi, [2, 3], wy, wy_s, True, qa, qa_s, 3, True, False)
+        carry(2)
+        quantize(3)
+        passes(y_lo, [0, 1], vo, vo_s, False, pw, pw_s, 3, False, True)
+        passes(y_hi, [2, 3], vo, vo_s, False, pw, pw_s, 3, False, True)
+        nc.vector.tensor_copy(out=y_sb[3][:, 0:2, :], in_=y_lo[:])
+        sy.dma_start(out=out_v[:, 0:2, cols(3)], in_=y_sb[3][:, 0:2, :])
+        nc.scalar.copy(out=y_sb[3][:, 2:4, :], in_=y_hi[:])
+        sc.dma_start(out=out_v[:, 2:4, cols(3)], in_=y_sb[3][:, 2:4, :])

@@ -42,7 +42,7 @@ def tile_mix_positive_scores_carry_rows_kernel(
         ka_s, kb_s, pw_s = byte_tile("ka_s", W), byte_tile("kb_s", W), byte_tile("pw_s", W)
         fi_sb = sb.tile([P, PACK], F32, name="fi_sb")
         pw_bf = [sb.tile([P, CH, PACK], BF16, name="pw_bf%d" % c, align_bytes=64) for c in range(4)]
-        y_sb = [sb.tile([P, 4, CH], F32, name="y_sb%d" % c) for c in range(4)]
+        y_sb = [sb.tile([P, 2 * CH], F32, name="y_sb%d" % u) for u in range(8)]
 
         def load_fp8(eng, tile, words):
             eng.dma_start(out=tile[:].bitcast(I32), in_=words[0].rearrange("p n t -> p (n t)").bitcast(I32))
@@ -59,15 +59,16 @@ def tile_mix_positive_scores_carry_rows_kernel(
 
         def regroup_words(dst, src):
             nc.vector.tensor_copy(
-                out=dst[:].rearrange("p (t m b) -> p t m b", t=PACK, b=2),
-                in_=src[:].rearrange("p (m t b) -> p t m b", t=PACK, b=2),
+                out=dst[:].bitcast(mybir.dt.uint16).rearrange("p (t m) -> p t m", t=PACK),
+                in_=src[:].bitcast(mybir.dt.uint16).rearrange("p (m t) -> p t m", t=PACK),
             )
 
         def regroup_scales(dst, src):
-            nc.vector.tensor_copy(
-                out=dst[:].rearrange("p (t m) -> p t m", t=PACK),
-                in_=src.rearrange("p (m t) -> p t m", t=PACK),
-            )
+            for t in (0, 2):
+                nc.vector.tensor_copy(
+                    out=dst[:].rearrange("p (t m) -> p t m", t=PACK)[:, t : t + 2, :],
+                    in_=src.rearrange("p (m t) -> p t m", t=PACK)[:, t : t + 2, :],
+                )
 
         def cols(c):
             return slice(CH * c, CH * (c + 1))
@@ -103,11 +104,20 @@ def tile_mix_positive_scores_carry_rows_kernel(
         stage = byte_tile("stage", 6 * W)
 
         def load_rows(eng, n, scales):
-            eng.dma_start(out=stage[0:16, W * n : W * (n + 1)].bitcast(I32), in_=scales[0].bitcast(I32))
+            eng.dma_start(out=stage[16:32, W * n : W * (n + 1)].bitcast(I32), in_=scales[0].bitcast(I32))
 
         def spread(eng, first, last, Q):
             span = slice(W * first, W * last)
-            eng.dma_start(out=planes[32 * Q : 32 * Q + 4, span].bitcast(I32), in_=stage[4 * Q : 4 * Q + 4, span].bitcast(I32))
+            eng.dma_start(out=planes[32 * Q : 32 * Q + 4, span].bitcast(I32), in_=stage[16 + 4 * Q : 20 + 4 * Q, span].bitcast(I32))
+
+        nc.vector.memset(pw[:, cols(0)].bitcast(I32), 0)
+        nc.vector.memset(pw_s[:, cols(0)].bitcast(I32), 0)
+        warm_bank = psum.tile([P, CH], F32, name="y3")
+        for n in range(36):
+            nc.tensor.matmul_mx(
+                out=warm_bank[:], lhsT=pw[:, cols(0)].bitcast(FP8X4), lhsT_scale=pw_s[:, cols(0)],
+                rhs=pw[:, cols(0)].bitcast(FP8X4), rhs_scale=pw_s[:, cols(0)], start=True, stop=True,
+            )
 
         nc.vector.memset(planes[:].bitcast(I32), 0)
         gp.dma_start(out=fi_sb[:], in_=fi.rearrange("(p t) o -> p (t o)", t=PACK))
@@ -116,8 +126,8 @@ def tile_mix_positive_scores_carry_rows_kernel(
         load_rows(sy, 2, kb_scales)
         load_rows(sc, 3, qb_scales)
         load_fp4(sy, ka_raw, ka_words)
-        load_fp8(sc, qa, qa_words)
-        load_fp4(sy, kb_raw, kb_words)
+        load_fp4(sc, kb_raw, kb_words)
+        load_fp8(sy, qa, qa_words)
         load_fp8(sc, qb, qb_words)
         for Q in range(4):
             spread(sy if Q % 2 == 0 else sc, 0, 4, Q)
@@ -129,45 +139,40 @@ def tile_mix_positive_scores_carry_rows_kernel(
             spread(sy, 4, 6, Q)
 
         a_bank = [psum.tile([P, PACK, CH], F32, name="a%d" % c) for c in range(4)]
-        y_bank = [psum.tile([P, 4, CH], F32, name="y%d" % c) for c in range(3)]
-        y_lo = psum.tile([P, 2, CH], F32, name="y3")
+
+        def scores(c):
+            passes(a_bank[c], ALL, ka, ka_s, True, qa, qa_s, c, True, False)
+            passes(a_bank[c], ALL, kb, kb_s, True, qb, qb_s, c, False, True)
+
+        def output(h, j):
+            bank = psum.tile([P, 2 * CH], F32, name=("y%d" if h == 0 else "a%d") % j)
+            half = slice(2 * CH * h, 2 * CH * (h + 1))
+            for n in range(2):
+                nc.tensor.matmul_mx(
+                    out=bank[:, cols(n)], lhsT=wy[:, 2 * P * j : 2 * P * (j + 1)].bitcast(FP4X4), lhsT_scale=wy_s[:, cols(j)],
+                    rhs=qa[:, cols(2 * h + n)].bitcast(FP8X4), rhs_scale=qa_s[:, cols(2 * h + n)], start=n == 0, stop=False,
+                )
+            nc.tensor.matmul_mx(
+                out=bank[:], lhsT=vo[:, cols(j)].bitcast(FP8X4), lhsT_scale=vo_s[:, cols(j)],
+                rhs=pw[:, half].bitcast(FP8X4), rhs_scale=pw_s[:, half], start=False, stop=True,
+            )
+            y = y_sb[4 * h + j]
+            if h == 1 and j % 2 == 1:
+                nc.vector.tensor_copy(out=y[:], in_=bank[:])
+            else:
+                nc.scalar.copy(out=y[:], in_=bank[:])
+            sy.dma_start(out=out[cols(j), half], in_=y[:])
 
         regroup_words(ka, ka_raw)
         regroup_words(kb, kb_raw)
         regroup_scales(ka_s, ka_s_raw)
         regroup_scales(kb_s, kb_s_raw)
         for c in range(4):
-            passes(a_bank[c], ALL, ka, ka_s, True, qa, qa_s, c, True, False)
-            passes(a_bank[c], ALL, kb, kb_s, True, qb, qb_s, c, False, True)
-
-        def skip(c):
-            passes(y_bank[c], ALL, wy, wy_s, True, qa, qa_s, c, True, False)
-
-        def carry(c):
-            passes(y_bank[c], ALL, vo, vo_s, False, pw, pw_s, c, False, True)
-            nc.scalar.copy(out=y_sb[c][:], in_=y_bank[c][:])
-            sy.dma_start(out=out_v[:, :, cols(c)], in_=y_sb[c][:])
-
-        weigh(0)
-        y_hi = psum.tile([P, 2, CH], F32, name="a0")
-        weigh(1)
-        quantize(0)
-        skip(0)
-        skip(1)
-        carry(0)
-        weigh(2)
-        quantize(1)
-        skip(2)
-        carry(1)
-        weigh(3)
-        quantize(2)
-        passes(y_lo, [0, 1], wy, wy_s, True, qa, qa_s, 3, True, False)
-        passes(y_hi, [2, 3], wy, wy_s, True, qa, qa_s, 3, True, False)
-        carry(2)
+            scores(c)
+            weigh(c)
+            if c > 0:
+                quantize(c - 1)
         quantize(3)
-        passes(y_lo, [0, 1], vo, vo_s, False, pw, pw_s, 3, False, True)
-        passes(y_hi, [2, 3], vo, vo_s, False, pw, pw_s, 3, False, True)
-        nc.vector.tensor_copy(out=y_sb[3][:, 0:2, :], in_=y_lo[:])
-        sy.dma_start(out=out_v[:, 0:2, cols(3)], in_=y_sb[3][:, 0:2, :])
-        nc.scalar.copy(out=y_sb[3][:, 2:4, :], in_=y_hi[:])
-        sc.dma_start(out=out_v[:, 2:4, cols(3)], in_=y_sb[3][:, 2:4, :])
+        for h in range(2):
+            for j in range(4):
+                output(h, j)

@@ -106,18 +106,22 @@ def tile_mix_positive_scores_carry_rows_kernel(
         def load_rows(eng, n, scales):
             eng.dma_start(out=stage[16:32, W * n : W * (n + 1)].bitcast(I32), in_=scales[0].bitcast(I32))
 
-        def spread(eng, first, last, Q):
+        def spread(eng, first, last, r):
             span = slice(W * first, W * last)
-            eng.dma_start(out=planes[32 * Q : 32 * Q + 4, span].bitcast(I32), in_=stage[16 + 4 * Q : 20 + 4 * Q, span].bitcast(I32))
+            eng.dma_start(out=planes[r:P:32, span].bitcast(I32), in_=stage[16 + r : 32 : 4, span].bitcast(I32))
 
         nc.vector.memset(pw[:, cols(0)].bitcast(I32), 0)
         nc.vector.memset(pw_s[:, cols(0)].bitcast(I32), 0)
         warm_bank = psum.tile([P, CH], F32, name="y3")
-        for n in range(36):
-            nc.tensor.matmul_mx(
-                out=warm_bank[:], lhsT=pw[:, cols(0)].bitcast(FP8X4), lhsT_scale=pw_s[:, cols(0)],
-                rhs=pw[:, cols(0)].bitcast(FP8X4), rhs_scale=pw_s[:, cols(0)], start=True, stop=True,
-            )
+
+        def warm_up(moving, count):
+            for n in range(count):
+                nc.tensor.matmul_mx(
+                    out=warm_bank[:], lhsT=pw[:, cols(0)].bitcast(FP8X4), lhsT_scale=pw_s[:, cols(0)],
+                    rhs=moving[:, cols(0)].bitcast(FP8X4), rhs_scale=pw_s[:, cols(0)], start=True, stop=True,
+                )
+
+        warm_up(pw, 20)
 
         nc.vector.memset(planes[:].bitcast(I32), 0)
         gp.dma_start(out=fi_sb[:], in_=fi.rearrange("(p t) o -> p (t o)", t=PACK))
@@ -137,6 +141,7 @@ def tile_mix_positive_scores_carry_rows_kernel(
         load_fp8(sy, vo, vo_words)
         for Q in range(4):
             spread(sy, 4, 6, Q)
+        warm_up(qb, 12)
 
         a_bank = [psum.tile([P, PACK, CH], F32, name="a%d" % c) for c in range(4)]
 
@@ -167,12 +172,12 @@ def tile_mix_positive_scores_carry_rows_kernel(
         regroup_words(kb, kb_raw)
         regroup_scales(ka_s, ka_s_raw)
         regroup_scales(kb_s, kb_s_raw)
-        for c in range(4):
-            scores(c)
-            weigh(c)
-            if c > 0:
-                quantize(c - 1)
-        quantize(3)
+        for h in range(2):
+            for c in (2 * h, 2 * h + 1):
+                scores(c)
+                weigh(c)
+            for c in (2 * h, 2 * h + 1):
+                quantize(c)
         for h in range(2):
             for j in range(4):
                 output(h, j)

@@ -121,7 +121,7 @@ def tile_mix_positive_scores_carry_rows_kernel(
                     rhs=moving[:, cols(0)].bitcast(FP8X4), rhs_scale=pw_s[:, cols(0)], start=True, stop=True,
                 )
 
-        warm_up(pw, 20)
+        warm_up(pw, 18)
 
         nc.vector.memset(planes[:].bitcast(I32), 0)
         gp.dma_start(out=fi_sb[:], in_=fi.rearrange("(p t) o -> p (t o)", t=PACK))
@@ -132,16 +132,16 @@ def tile_mix_positive_scores_carry_rows_kernel(
         load_fp4(sy, ka_raw, ka_words)
         load_fp4(sc, kb_raw, kb_words)
         load_fp8(sy, qa, qa_words)
-        load_fp8(sc, qb, qb_words)
+        load_rows(sc, 4, wy_scales)
         for Q in range(4):
             spread(sy if Q % 2 == 0 else sc, 0, 4, Q)
-        load_rows(sy, 4, wy_scales)
+        load_fp8(sy, qb, qb_words)
         load_rows(sy, 5, vo_scales)
         load_fp4(sy, wy, wy_words)
         load_fp8(sy, vo, vo_words)
         for Q in range(4):
             spread(sy, 4, 6, Q)
-        warm_up(qb, 12)
+        warm_up(qa, 10)
 
         a_bank = [psum.tile([P, PACK, CH], F32, name="a%d" % c) for c in range(4)]
 
@@ -162,7 +162,7 @@ def tile_mix_positive_scores_carry_rows_kernel(
                 rhs=pw[:, half].bitcast(FP8X4), rhs_scale=pw_s[:, half], start=False, stop=True,
             )
             y = y_sb[4 * h + j]
-            if h == 1 and j % 2 == 1:
+            if 4 * h + j >= 3 and j % 2 == 1:
                 nc.vector.tensor_copy(out=y[:], in_=bank[:])
             else:
                 nc.scalar.copy(out=y[:], in_=bank[:])

from contextlib import ExitStack

import concourse.mybir as mybir

F32 = mybir.dt.float32
BF16 = mybir.dt.bfloat16
I32 = mybir.dt.int32
U32 = mybir.dt.uint32
U8 = mybir.dt.uint8
FP8X4 = mybir.dt.float8_e4m3fn_x4
FP4X4 = mybir.dt.float4_e2m1fn_x4
ALU = mybir.AluOpType

P = 128
W = 512
PACK = 4
CH = 128
FLOPS = 4 * 2 * 512 * 512 * 512


def tile_mix_positive_scores_carry_rows_kernel(
    tc, qa_words, qa_scales, ka_words, ka_scales, qb_words, qb_scales, kb_words, kb_scales,
    fi, vo_words, vo_scales, wy_words, wy_scales, out,
):
    nc = tc.nc
    with ExitStack() as ctx:
        sb = ctx.enter_context(tc.tile_pool(name="sb", bufs=1))
        psum = ctx.enter_context(tc.psum_pool(name="psum", bufs=1))
        ctx.enter_context(tc.manual_schedule())

        def fp8_tile(name):
            return sb.tile([P, W], U32, name=name, align_bytes=64)

        def byte_tile(name, width):
            return sb.tile([P, width], U8, name=name, align_bytes=64)

        qa, qb, vo, pw = fp8_tile("qa"), fp8_tile("qb"), fp8_tile("vo"), fp8_tile("pw")
        ka_raw, kb_raw, wy = byte_tile("ka_raw", 2 * W), byte_tile("kb_raw", 2 * W), byte_tile("wy", 2 * W)
        ka, kb = byte_tile("ka", 2 * W), byte_tile("kb", 2 * W)
        planes = byte_tile("planes", 6 * W)
        ka_s_raw, qa_s, kb_s_raw, qb_s, wy_s, vo_s = [planes[:, W * n : W * (n + 1)] for n in range(6)]
        ka_s, kb_s, pw_s = byte_tile("ka_s", W), byte_tile("kb_s", W), byte_tile("pw_s", W)
        fi_sb = sb.tile([P, PACK], F32, name="fi_sb")
        pw_bf = [sb.tile([P, CH, PACK], BF16, name="pw_bf%d" % c, align_bytes=64) for c in range(4)]
        y_sb = [sb.tile([P, 2 * CH], F32, name="y_sb%d" % u) for u in range(8)]

        def load_fp8(eng, tile, words):
            eng.dma_start(out=tile[:].bitcast(I32), in_=words[0].rearrange("p n t -> p (n t)").bitcast(I32))

        def load_fp4(eng, tile, words):
            eng.dma_start(out=tile[:].bitcast(I32), in_=words[0].bitcast(I32))

        def load_scale(eng, plane, scales, r):
            eng.dma_start(out=plane.bitcast(I32)[r:P:32, :], in_=scales[0].bitcast(I32)[r:16:4, :])

        def load_scale_all(eng, plane, scales):
            src = scales[0].bitcast(I32).rearrange("(Q r) c -> Q (r c)", r=4).unsqueeze(1).to_broadcast([4, 8, W])
            eng.dma_start(out=plane.bitcast(I32), in_=src)

        def regroup_words(dst, src):
            nc.vector.tensor_copy(
                out=dst[:].bitcast(mybir.dt.uint16).rearrange("p (t m) -> p t m", t=PACK),
                in_=src[:].bitcast(mybir.dt.uint16).rearrange("p (m t) -> p t m", t=PACK),
            )

        def regroup_scales(dst, src):
            for t in (0, 2):
                nc.vector.tensor_copy(
                    out=dst[:].rearrange("p (t m) -> p t m", t=PACK)[:, t : t + 2, :],
                    in_=src.rearrange("p (m t) -> p t m", t=PACK)[:, t : t + 2, :],
                )

        def cols(c):
            return slice(CH * c, CH * (c + 1))

        def passes(bank, js, w, w_s, w_fp4, x, x_s, c, start, stop):
            for n, j in enumerate(js):
                if w_fp4:
                    lhsT = w[:, 2 * P * j : 2 * P * (j + 1)].bitcast(FP4X4)
                else:
                    lhsT = w[:, cols(j)].bitcast(FP8X4)
                nc.tensor.matmul_mx(
                    out=bank[:, n, :], lhsT=lhsT, lhsT_scale=w_s[:, cols(j)],
                    rhs=x[:, cols(c)].bitcast(FP8X4), rhs_scale=x_s[:, cols(c)],
                    start=start and n == 0, stop=stop and n == len(js) - 1,
                )

        def weigh(c):
            nc.vector.scalar_tensor_tensor(
                out=pw_bf[c][:], in0=a_bank[c][:].rearrange("p t q -> p q t"), scalar=0.0,
                in1=fi_sb[:].unsqueeze(1).to_broadcast([P, CH, PACK]), op0=ALU.max, op1=ALU.mult,
            )

        def quantize(c):
            nc.vector.quantize_mx(
                out=pw[:, cols(c)].bitcast(FP8X4), scales=pw_s[:, cols(c)],
                in_=pw_bf[c][:].rearrange("p q t -> p (q t)"),
            )

        out_v = out.rearrange("(j p) q -> p j q", p=P)
        sy, sc, gp = nc.sync, nc.scalar, nc.gpsimd
        ALL = [0, 1, 2, 3]

        stage = byte_tile("stage", 6 * W)

        def load_rows(eng, n, scales):
            eng.dma_start(out=stage[16:32, W * n : W * (n + 1)].bitcast(I32), in_=scales[0].bitcast(I32))

        def spread(eng, first, last, r):
            span = slice(W * first, W * last)
            eng.dma_start(out=planes[r:P:32, span].bitcast(I32), in_=stage[16 + r : 32 : 4, span].bitcast(I32))

        nc.vector.memset(pw[:, cols(0)].bitcast(I32), 0)
        nc.vector.memset(pw_s[:, cols(0)].bitcast(I32), 0)
        warm_bank = psum.tile([P, CH], F32, name="y3")

        def warm_up(moving, count):
            for n in range(count):
                nc.tensor.matmul_mx(
                    out=warm_bank[:], lhsT=pw[:, cols(0)].bitcast(FP8X4), lhsT_scale=pw_s[:, cols(0)],
                    rhs=moving[:, cols(0)].bitcast(FP8X4), rhs_scale=pw_s[:, cols(0)], start=True, stop=True,
                )

        warm_up(pw, 18)

        nc.vector.memset(planes[:].bitcast(I32), 0)
        gp.dma_start(out=fi_sb[:], in_=fi.rearrange("(p t) o -> p (t o)", t=PACK))
        load_rows(sy, 0, ka_scales)
        load_rows(sc, 1, qa_scales)
        load_rows(sy, 2, kb_scales)
        load_rows(sc, 3, qb_scales)
        load_fp4(sy, ka_raw, ka_words)
        load_fp4(sc, kb_raw, kb_words)
        load_fp8(sy, qa, qa_words)
        load_rows(sc, 4, wy_scales)
        for Q in range(4):
            spread(sy if Q % 2 == 0 else sc, 0, 4, Q)
        load_fp8(sy, qb, qb_words)
        load_rows(sy, 5, vo_scales)
        load_fp4(sy, wy, wy_words)
        load_fp8(sy, vo, vo_words)
        for Q in range(4):
            spread(sy, 4, 6, Q)
        warm_up(qa, 10)

        a_bank = [psum.tile([P, PACK, CH], F32, name="a%d" % c) for c in range(4)]

        def scores(c):
            passes(a_bank[c], ALL, ka, ka_s, True, qa, qa_s, c, True, False)
            passes(a_bank[c], ALL, kb, kb_s, True, qb, qb_s, c, False, True)

        def output(h, j):
            bank = psum.tile([P, 2 * CH], F32, name=("y%d" if h == 0 else "a%d") % j)
            half = slice(2 * CH * h, 2 * CH * (h + 1))
            for n in range(2):
                nc.tensor.matmul_mx(
                    out=bank[:, cols(n)], lhsT=wy[:, 2 * P * j : 2 * P * (j + 1)].bitcast(FP4X4), lhsT_scale=wy_s[:, cols(j)],
                    rhs=qa[:, cols(2 * h + n)].bitcast(FP8X4), rhs_scale=qa_s[:, cols(2 * h + n)], start=n == 0, stop=False,
                )
            nc.tensor.matmul_mx(
                out=bank[:], lhsT=vo[:, cols(j)].bitcast(FP8X4), lhsT_scale=vo_s[:, cols(j)],
                rhs=pw[:, half].bitcast(FP8X4), rhs_scale=pw_s[:, half], start=False, stop=True,
            )
            y = y_sb[4 * h + j]
            if 4 * h + j >= 3 and j % 2 == 1:
                nc.vector.tensor_copy(out=y[:], in_=bank[:])
            else:
                nc.scalar.copy(out=y[:], in_=bank[:])
            sy.dma_start(out=out[cols(j), half], in_=y[:])

        regroup_words(ka, ka_raw)
        regroup_words(kb, kb_raw)
        regroup_scales(ka_s, ka_s_raw)
        regroup_scales(kb_s, kb_s_raw)
        for h in range(2):
            for c in (2 * h, 2 * h + 1):
                scores(c)
                weigh(c)
            for c in (2 * h, 2 * h + 1):
                quantize(c)
        for h in range(2):
            for j in range(4):
                output(h, j)
